import numpy as np
import ml_dtypes


def mxq(x, axis, fmt="e4m3"):
    dtype, down = {"e4m3": (ml_dtypes.float8_e4m3fn, 7), "e5m2": (ml_dtypes.float8_e5m2, 14)}[fmt]
    v = np.moveaxis(np.asarray(x, np.float32).astype(ml_dtypes.bfloat16).astype(np.float64), axis, -1)
    blocks = v.reshape(v.shape[:-1] + (-1, 32))
    amax = np.abs(blocks).max(-1, keepdims=True)
    byte = np.maximum(np.where(amax > 0, np.frexp(amax)[1] - 1 + 127, 0) - down, 1)
    scale = np.exp2(byte - 127.0)
    codes = (blocks / scale).astype(np.float32).astype(dtype).astype(np.float64)
    return np.moveaxis((codes * scale).reshape(v.shape), -1, axis)


WIDE = False


def mx_kscale(k):
    if not WIDE:
        return np.ones(k)
    levels = np.array([10, -10, 5, -5, 0])
    if k % 512:
        return np.exp2(np.random.permutation(np.resize(levels, k // 32))).repeat(32)
    a = np.empty((k // 512, 16))
    for p in range(k // 512):
        a[p, :8] = np.random.permutation(np.resize(levels, 8))
        for g in range(8):
            far = levels[np.abs(levels - a[p, g]) >= 10]
            a[p, g + 8] = far[np.random.randint(len(far))]
    return np.exp2(a.ravel()).repeat(32)


def f64(x):
    return np.asarray(x).astype(np.float64)


def striped(idx):
    return np.tile(idx.reshape(-1, 16).T, (8, 1)).astype(np.uint16)


def unstriped(offs):
    return offs[:16].T.reshape(-1).astype(np.int64)


def striped8(idx):
    return np.concatenate([x.reshape(-1, 16).T for x in idx]).astype(np.uint16)


def runs(offs, k):
    lists = np.stack([offs[16 * r : 16 * r + 16].T.reshape(-1) for r in range(8)]).astype(np.int64)
    return lists[np.arange(k) % 512 // 64]


def pack_weight(w):
    k, n = w.shape
    w = f64(np.asarray(w, np.float32).astype(ml_dtypes.bfloat16)).reshape(k // 32, 32, n)
    amax = np.abs(w).max(1)
    byte = np.clip(np.where(amax > 0, np.frexp(amax)[1] - 1 + 127 - 7, 1), 1, 254)
    scaled = (w * np.exp2(127.0 - byte)[:, None, :]).reshape(k, n).astype(np.float32)
    words = np.ascontiguousarray(scaled.reshape(k // 512, 128, 4, n).transpose(0, 1, 3, 2)).astype(ml_dtypes.float8_e4m3fn).view(np.uint8)
    return words, np.ascontiguousarray(byte.astype(np.uint8).reshape(k // 512, 16, n))


def unpack_weight(words, scales):
    g, p, n, _ = words.shape
    vals = np.ascontiguousarray(words).view(ml_dtypes.float8_e4m3fn).astype(np.float64) * np.repeat(np.exp2(scales.astype(np.float64) - 127.0), 8, axis=1)[..., None]
    return vals.transpose(0, 1, 3, 2).reshape(g * 512, n)


E2M1 = np.array([0.0, 0.5, 1.0, 1.5, 2.0, 3.0, 4.0, 6.0, -0.0, -0.5, -1.0, -1.5, -2.0, -3.0, -4.0, -6.0])


def pack_fp4(w):
    k, n = w.shape
    w = f64(np.asarray(w, np.float32).astype(ml_dtypes.bfloat16)).reshape(k // 32, 32, n)
    amax = np.abs(w).max(1)
    mant, ex = np.frexp(amax / 6.0)
    byte = np.clip(np.where(amax > 0, np.where(mant > 0.5, ex, ex - 1) + 127, 1), 1, 254)
    scaled = (w * np.exp2(127.0 - byte)[:, None, :]).reshape(k, n).astype(np.float32)
    c = np.ascontiguousarray(scaled.reshape(k // 512, 128, 4, n).transpose(0, 1, 3, 2)).astype(ml_dtypes.float4_e2m1fn).view(np.uint8) & 0xF
    words = (c[..., 0::2] | (c[..., 1::2] << 4)).reshape(k // 512, 128, 2 * n)
    return np.ascontiguousarray(words), np.ascontiguousarray(byte.astype(np.uint8).reshape(k // 512, 16, n))


def unpack_fp4(words, scales):
    g, _, n = scales.shape
    words = np.ascontiguousarray(words).reshape(g, 128, n, 2)
    nib = np.empty((g, 128, n, 4), np.uint8)
    nib[..., 0::2] = words & 0xF
    nib[..., 1::2] = words >> 4
    vals = E2M1[nib] * np.repeat(np.exp2(scales.astype(np.float64) - 127.0), 8, axis=1)[..., None]
    return vals.transpose(0, 1, 3, 2).reshape(g * 512, n)


def planes(y):
    n, m = y.shape
    v = y.astype(np.float32).astype(ml_dtypes.bfloat16).astype(np.float64).reshape(n // 32, 32, m)
    top = np.abs(v).max(1)
    byte = np.clip(np.where(top > 0, np.frexp(top)[1] - 1 + 127 - 7, 1), 1, 254)
    codes = (v * np.exp2(127.0 - byte)[:, None, :]).reshape(n, m).astype(np.float32).astype(ml_dtypes.float8_e4m3fn).view(np.uint8)
    words = codes.reshape(n // 512, 128, 4, m).transpose(0, 1, 3, 2)
    return np.ascontiguousarray(words), np.ascontiguousarray(byte.astype(np.uint8).reshape(n // 512, 16, m))


K, T, S, H, G = 512, 1024, 512, 512, 2048


def setup_inputs():
    n = np.random.standard_normal
    s = mx_kscale(K)[:, None]
    packed_xT = pack_weight(n((K, T)) * s)
    packed_w1 = pack_fp4(n((K, H)) / np.sqrt(K) / s)
    packed_w2 = pack_fp4(n((K, H)) / np.sqrt(K) / s)
    packed_dT = pack_weight(n((K, G)) / s)
    return {
        "x_words": packed_xT[0],
        "x_scales": packed_xT[1],
        "w1_words": packed_w1[0],
        "w1_scales": packed_w1[1],
        "w2_words": packed_w2[0],
        "w2_scales": packed_w2[1],
        "gs": (np.random.uniform(0.5, 1.5, (K, 1)) * s).astype(np.float32),
        "d_words": packed_dT[0],
        "d_scales": packed_dT[1],
        "offs": striped(np.random.permutation(T)[:S]),
        "two": striped(np.random.permutation(T)[:S]),
        "n1": striped8(np.stack([np.random.permutation(S) for _ in range(8)])),
        "n2": striped8(np.stack([np.random.permutation(S) for _ in range(8)])),
        "n3": striped8(np.stack([np.random.permutation(S) for _ in range(8)])),
        "n4": striped8(np.stack([np.random.permutation(S) for _ in range(8)])),
        "k1": striped8(np.random.randint(0, G, (8, H))),
        "n5": striped8(np.stack([np.random.permutation(S) for _ in range(8)])),
        "n6": striped8(np.stack([np.random.permutation(S) for _ in range(8)])),
        "n7": striped8(np.stack([np.random.permutation(S) for _ in range(8)])),
    }


def reference(x_words, x_scales, w1_words, w1_scales, w2_words, w2_scales, gs, d_words, d_scales, offs, two, n1, n2, n3, n4, k1, n5, n6, n7):
    d_k1 = unpack_weight(d_words, d_scales)[np.arange(K)[:, None], runs(k1, K)]
    xq = unpack_weight(x_words, x_scales)[:, unstriped(offs)]
    y = unpack_fp4(w1_words, w1_scales).T @ xq
    x_two = unpack_weight(x_words, x_scales)[:, unstriped(two)]
    d = unpack_fp4(w2_words, w2_scales).T @ x_two
    z = f64(gs) * (np.maximum(y[np.arange(H)[:, None], runs(n1, H)] + d[np.arange(H)[:, None], runs(n3, H)], y[np.arange(H)[:, None], runs(n2, H)] + d[np.arange(H)[:, None], runs(n4, H)]))
    h = 0.0625 * ((d_k1.T @ mxq(z, 0, "e4m3")))
    out_0 = 0.75 * (h * (h[np.arange(H)[:, None], runs(n5, H)]) + (h[np.arange(H)[:, None], runs(n6, H)]) * (h[np.arange(H)[:, None], runs(n7, H)]))
    return (out_0,) + planes(out_0)

@@ -1,0 +1,227 @@
+from contextlib import ExitStack
+
+import concourse.mybir as mybir
+
+K, T, S, H, G = 512, 1024, 512, 512, 2048
+FLOPS = 3 * 2 * K * H * S
+
+F32 = mybir.dt.float32
+BF16 = mybir.dt.bfloat16
+I32 = mybir.dt.int32
+U32 = mybir.dt.uint32
+U16 = mybir.dt.uint16
+U8 = mybir.dt.uint8
+FP8X4 = mybir.dt.float8_e4m3fn_x4
+FP4X4 = mybir.dt.float4_e2m1fn_x4
+ADD = mybir.AluOpType.add
+MULT = mybir.AluOpType.mult
+MAX = mybir.AluOpType.max
+COPY = mybir.ActivationFunctionType.Copy
+
+P = 128
+PACK = 4
+CHUNKS = ((0, 256), (256, 128), (384, 128))
+
+
+def tile_picked_twqpathbdot_none_po_kernel(
+    tc, x_words, x_scales, w1_words, w1_scales, w2_words, w2_scales, gs, d_words, d_scales,
+    offs, two, n1, n2, n3, n4, k1, n5, n6, n7, out_0, out_1, out_2,
+):
+    nc = tc.nc
+    with ExitStack() as ctx:
+        lists = ctx.enter_context(tc.tile_pool(name="lists", bufs=1))
+        keep = ctx.enter_context(tc.tile_pool(name="keep", bufs=1))
+        psum = ctx.enter_context(tc.psum_pool(name="psum", bufs=1))
+
+        def tile(shape, dtype, name):
+            return keep.tile(shape, dtype, name=name, align_bytes=64)
+
+        def bank(b, shape):
+            return psum.tile(shape, F32, name="bank%d" % b, tag="bank%d" % b)
+
+        def load_list(src, name):
+            dst = lists.tile([P, S // 16], U16, name=name)
+            nc.sync.dma_start(dst[:], src)
+            return dst
+
+        def load_scales(dst, src):
+            for q in range(4):
+                nc.sync.dma_start(dst[32 * q : 32 * q + 4, :].bitcast(I32), src[0, 4 * q : 4 * q + 4, :].bitcast(I32))
+
+        def entries(lst, c0, n):
+            return lst[:, c0 // 16 : (c0 + n) // 16]
+
+        xs = tile([P, T], U8, "xs")
+        w1s = tile([P, H], U8, "w1s")
+        w2s = tile([P, H], U8, "w2s")
+        ds = tile([P, G], U8, "ds")
+        ds_placed = tile([P, H], U8, "ds_placed")
+        nc.vector.memset(xs[:].bitcast(I32), 0)
+        nc.vector.memset(w1s[:].bitcast(I32), 0)
+        nc.vector.memset(w2s[:].bitcast(I32), 0)
+        nc.vector.memset(ds[:].bitcast(I32), 0)
+        nc.vector.memset(ds_placed[:].bitcast(I32), 0)
+
+        xw = tile([P, T], I32, "xw")
+        w1w = tile([P, 2 * H], U8, "w1w")
+        w2w = tile([P, 2 * H], U8, "w2w")
+        dw = tile([P, G], I32, "dw")
+        gains = tile([P, PACK], F32, "gains")
+
+        nc.sync.dma_start(xw[:], x_words[0].rearrange("p n t -> p (n t)").bitcast(I32))
+        l_offs = load_list(offs, "l_offs")
+        nc.sync.dma_start(w1w[:].bitcast(I32), w1_words[0].bitcast(I32))
+        l_two = load_list(two, "l_two")
+        load_scales(xs, x_scales)
+        load_scales(w1s, w1_scales)
+        l1 = load_list(n1, "l1")
+        l2 = load_list(n2, "l2")
+        nc.sync.dma_start(w2w[:].bitcast(I32), w2_words[0].bitcast(I32))
+        load_scales(w2s, w2_scales)
+        l3 = load_list(n3, "l3")
+        l4 = load_list(n4, "l4")
+        nc.sync.dma_start(gains[:], gs.rearrange("(p t) o -> p (t o)", t=PACK))
+        lk = load_list(k1, "lk")
+        for r in range(4):
+            first = 16 * (r // 2) + r % 2
+            nc.sync.dma_start(ds[first:P:32, :].bitcast(I32), d_scales[0, r:16:4, :].bitcast(I32))
+        nc.sync.dma_start(dw[:], d_words[0].rearrange("p n t -> p (n t)").bitcast(I32))
+        l5 = load_list(n5, "l5")
+        l6 = load_list(n6, "l6")
+        l7 = load_list(n7, "l7")
+
+        def deal(src, width, dtype, name):
+            dst = tile([P, H * width], dtype, name)
+            nc.vector.tensor_copy(
+                dst[:].rearrange("p (t m b) -> p t m b", t=PACK, b=width),
+                src.rearrange("p (m t b) -> p t m b", t=PACK, b=width),
+            )
+            return dst
+
+        def project(lst, ww, ws, first_bank, name):
+            words = tile([P, S], U32, name + "_xw")
+            nc.vector.tensor_copy(words[:], xw[:].bitcast(U32).indirect(lst[:]))
+            w_words = deal(ww[:], 2, U8, name + "_ww")
+            scales = tile([P, S], U8, name + "_xs")
+            nc.vector.tensor_copy(scales[:], xs[:].indirect(lst[:]))
+            w_scales = deal(ws[:], 1, U8, name + "_ws")
+            rows = []
+            for t in range(PACK):
+                acc = bank(first_bank + t, [P, S])
+                nc.tensor.matmul_mx(
+                    acc[:],
+                    lhsT=w_words[:, 2 * P * t : 2 * P * (t + 1)].bitcast(FP4X4),
+                    lhsT_scale=w_scales[:, P * t : P * (t + 1)],
+                    rhs=words[:].bitcast(FP8X4),
+                    rhs_scale=scales[:],
+                    start=True,
+                    stop=True,
+                )
+                row = tile([P, S], F32, "%s%d" % (name, t))
+                nc.scalar.copy(row[:], acc[:])
+                rows.append(row)
+            return rows
+
+        y = project(l_offs, w1w, w1s, 0, "y")
+        d = project(l_two, w2w, w2s, 4, "d")
+
+        z_words = tile([P, S], U32, "z_words")
+        z_scales = tile([P, S], U8, "z_scales")
+
+        def mix(c0, n):
+            ya = tile([P, PACK, n], F32, "ya%d" % c0)
+            yb = tile([P, PACK, n], F32, "yb%d" % c0)
+            sa = tile([P, PACK, n], F32, "sa%d" % c0)
+            sb = tile([P, PACK, n], F32, "sb%d" % c0)
+            top = tile([P, PACK, n], F32, "top%d" % c0)
+            planes = tile([P, PACK, n], BF16, "planes%d" % c0)
+            woven = tile([P, n, PACK], BF16, "woven%d" % c0)
+            for t in range(PACK):
+                nc.vector.tensor_copy(ya[:, t, :], y[t][:].indirect(entries(l1, c0, n)))
+                nc.vector.tensor_copy(yb[:, t, :], y[t][:].indirect(entries(l2, c0, n)))
+            for t in range(PACK + 1):
+                if t < PACK:
+                    nc.vector.tensor_tensor(sa[:, t, :], d[t][:].indirect(entries(l3, c0, n)), ya[:, t, :], ADD)
+                    nc.vector.tensor_tensor(sb[:, t, :], d[t][:].indirect(entries(l4, c0, n)), yb[:, t, :], ADD)
+                if t > 0:
+                    u = t - 1
+                    nc.vector.tensor_tensor(top[:, u, :], sa[:, u, :], sb[:, u, :], MAX)
+                    nc.scalar.activation(planes[:, u, :], top[:, u, :], COPY, scale=gains[:, u : u + 1])
+            nc.scalar.copy(woven[:], planes[:].rearrange("p t j -> p j t"))
+            return woven
+
+        def quantise(woven, words, scales, c0, n):
+            nc.vector.quantize_mx(words[:, c0 : c0 + n].bitcast(FP8X4), scales[:, c0 : c0 + n], woven[:].rearrange("p j t -> p (j t)"))
+
+        woven_z = [mix(*CHUNKS[0])]
+
+        dk_scales = tile([P, H], U8, "dk_scales")
+        nc.vector.tensor_copy(dk_scales[:], ds[:].indirect(lk[:]))
+        dk_scales_dealt = deal(dk_scales[:], 1, U8, "dk_scales_dealt")
+        for r in range(4):
+            first = 16 * (r // 2) + r % 2
+            nc.sync.dma_start(ds_placed[r:P:32, :].bitcast(I32), dk_scales_dealt[first:P:32, :].bitcast(I32))
+        dk_words = tile([P, H], U32, "dk_words")
+        nc.vector.tensor_copy(dk_words[:], dw[:].bitcast(U32).indirect(lk[:]))
+        dk = deal(dk_words[:].bitcast(I32), 1, I32, "dk")
+
+        h = [tile([P, S], F32, "h%d" % t) for t in range(PACK)]
+        hs = [tile([P, S], F32, "hs%d" % t) for t in range(PACK)]
+
+        def layer(i):
+            c0, n = CHUNKS[i]
+            quantise(woven_z[i], z_words, z_scales, c0, n)
+            per_bank = 512 // n
+            accs = [bank(2 * i + b, [P, per_bank, n]) for b in range(PACK // per_bank)]
+            for t in range(PACK):
+                nc.tensor.matmul_mx(
+                    accs[t // per_bank][:, t % per_bank, :],
+                    lhsT=dk[:, P * t : P * (t + 1)].bitcast(FP8X4),
+                    lhsT_scale=ds_placed[:, P * t : P * (t + 1)],
+                    rhs=z_words[:, c0 : c0 + n].bitcast(FP8X4),
+                    rhs_scale=z_scales[:, c0 : c0 + n],
+                    start=True,
+                    stop=True,
+                )
+            for t in range(PACK):
+                acc = accs[t // per_bank][:, t % per_bank, :]
+                nc.scalar.activation(hs[t][:, c0 : c0 + n], acc, COPY, scale=0.75 * 0.0625)
+                nc.scalar.activation(h[t][:, c0 : c0 + n], acc, COPY, scale=0.0625)
+
+        for i in range(1, len(CHUNKS)):
+            woven_z.append(mix(*CHUNKS[i]))
+            layer(i - 1)
+        layer(len(CHUNKS) - 1)
+
+        o_words = tile([P, S], U32, "o_words")
+        o_scales = tile([P, S], U8, "o_scales")
+        out_rows = out_0.rearrange("(p t) j -> p t j", t=PACK)
+        out_words = out_1[0].rearrange("p n t -> p (n t)").bitcast(I32)
+
+        def products(c0, n):
+            h6 = tile([P, PACK, n], F32, "h6_%d" % c0)
+            pa = tile([P, PACK, n], F32, "pa%d" % c0)
+            pb = tile([P, PACK, n], F32, "pb%d" % c0)
+            res = tile([P, PACK, n], F32, "res%d" % c0)
+            woven = tile([P, n, PACK], BF16, "owoven%d" % c0)
+            for t in range(PACK):
+                nc.vector.tensor_copy(h6[:, t, :], hs[t][:].indirect(entries(l6, c0, n)))
+                nc.vector.tensor_tensor(pa[:, t, :], h[t][:].indirect(entries(l5, c0, n)), hs[t][:, c0 : c0 + n], MULT)
+            for t in range(PACK):
+                nc.vector.tensor_tensor(pb[:, t, :], h[t][:].indirect(entries(l7, c0, n)), h6[:, t, :], MULT)
+            nc.vector.tensor_tensor(res[:], pa[:], pb[:], ADD)
+            nc.sync.dma_start(out_rows[:, :, c0 : c0 + n], res[:])
+            nc.scalar.copy(woven[:], res[:].rearrange("p t j -> p j t"))
+            return woven
+
+        def hand_on(woven, c0, n):
+            quantise(woven, o_words, o_scales, c0, n)
+            nc.sync.dma_start(out_words[:, c0 : c0 + n], o_words[:, c0 : c0 + n].bitcast(I32))
+
+        woven_o = [products(*CHUNKS[0])]
+        for i in range(1, len(CHUNKS)):
+            woven_o.append(products(*CHUNKS[i]))
+            hand_on(woven_o[i - 1], *CHUNKS[i - 1])
+        hand_on(woven_o[-1], *CHUNKS[-1])
+        for q in range(4):
+            nc.sync.dma_start(out_2[0, 4 * q : 4 * q + 4, :].bitcast(I32), o_scales[32 * q : 32 * q + 4, :].bitcast(I32))

@@ -1,6 +1,8 @@
+import math
 from contextlib import ExitStack
 
 import concourse.mybir as mybir
+from concourse.masks import make_identity
 
 K, T, S, H, G = 512, 1024, 512, 512, 2048
 FLOPS = 3 * 2 * K * H * S
@@ -14,13 +16,19 @@ U8 = mybir.dt.uint8
 FP8X4 = mybir.dt.float8_e4m3fn_x4
 FP4X4 = mybir.dt.float4_e2m1fn_x4
 ADD = mybir.AluOpType.add
-MULT = mybir.AluOpType.mult
+SUB = mybir.AluOpType.subtract
 MAX = mybir.AluOpType.max
+MULT = mybir.AluOpType.mult
+RELU = mybir.ActivationFunctionType.Relu
 COPY = mybir.ActivationFunctionType.Copy
 
+H_SCALE = 0.0625 * math.sqrt(0.75)
 P = 128
 PACK = 4
 CHUNKS = ((0, 256), (256, 128), (384, 128))
+LAST = S - P
+HALF = S // 2
+WHOLE = 2
 
 
 def tile_picked_twqpathbdot_none_po_kernel(
@@ -31,6 +39,8 @@ def tile_picked_twqpathbdot_none_po_kernel(
     with ExitStack() as ctx:
         lists = ctx.enter_context(tc.tile_pool(name="lists", bufs=1))
         keep = ctx.enter_context(tc.tile_pool(name="keep", bufs=1))
+        ring = ctx.enter_context(tc.tile_pool(name="ring", bufs=4))
+        pairs = ctx.enter_context(tc.tile_pool(name="pairs", bufs=2))
         psum = ctx.enter_context(tc.psum_pool(name="psum", bufs=1))
 
         def tile(shape, dtype, name):
@@ -52,15 +62,18 @@ def tile_picked_twqpathbdot_none_po_kernel(
             return lst[:, c0 // 16 : (c0 + n) // 16]
 
         xs = tile([P, T], U8, "xs")
-        w1s = tile([P, H], U8, "w1s")
+        w1s = keep.tile([P, H], U8, name="w1s", tag="d_xs", align_bytes=64)
         w2s = tile([P, H], U8, "w2s")
         ds = tile([P, G], U8, "ds")
         ds_placed = tile([P, H], U8, "ds_placed")
-        nc.vector.memset(xs[:].bitcast(I32), 0)
-        nc.vector.memset(w1s[:].bitcast(I32), 0)
-        nc.vector.memset(w2s[:].bitcast(I32), 0)
-        nc.vector.memset(ds[:].bitcast(I32), 0)
-        nc.vector.memset(ds_placed[:].bitcast(I32), 0)
+        nc.gpsimd.memset(xs[:].bitcast(I32), 0)
+        nc.gpsimd.memset(w1s[:].bitcast(I32), 0)
+        nc.gpsimd.memset(w2s[:].bitcast(I32), 0)
+        nc.gpsimd.memset(ds[:].bitcast(I32), 0)
+        nc.gpsimd.memset(ds_placed[:].bitcast(I32), 0)
+
+        ident = tile([P, P], F32, "ident")
+        make_identity(nc, ident[:])
 
         xw = tile([P, T], I32, "xw")
         w1w = tile([P, 2 * H], U8, "w1w")
@@ -68,18 +81,18 @@ def tile_picked_twqpathbdot_none_po_kernel(
         dw = tile([P, G], I32, "dw")
         gains = tile([P, PACK], F32, "gains")
 
-        nc.sync.dma_start(xw[:], x_words[0].rearrange("p n t -> p (n t)").bitcast(I32))
         l_offs = load_list(offs, "l_offs")
         nc.sync.dma_start(w1w[:].bitcast(I32), w1_words[0].bitcast(I32))
+        nc.sync.dma_start(xw[:], x_words[0].rearrange("p n t -> p (n t)").bitcast(I32))
         l_two = load_list(two, "l_two")
         load_scales(xs, x_scales)
         load_scales(w1s, w1_scales)
-        l1 = load_list(n1, "l1")
-        l2 = load_list(n2, "l2")
         nc.sync.dma_start(w2w[:].bitcast(I32), w2_words[0].bitcast(I32))
         load_scales(w2s, w2_scales)
-        l3 = load_list(n3, "l3")
+        l2 = load_list(n2, "l2")
         l4 = load_list(n4, "l4")
+        l1 = load_list(n1, "l1")
+        l3 = load_list(n3, "l3")
         nc.sync.dma_start(gains[:], gs.rearrange("(p t) o -> p (t o)", t=PACK))
         lk = load_list(k1, "lk")
         for r in range(4):
@@ -90,22 +103,32 @@ def tile_picked_twqpathbdot_none_po_kernel(
         l6 = load_list(n6, "l6")
         l7 = load_list(n7, "l7")
 
-        def deal(src, width, dtype, name):
-            dst = tile([P, H * width], dtype, name)
+        def deal(src, width, run, dtype, name):
+            dst = keep.tile([P, H * width], dtype, name=name, tag=name, align_bytes=64)
             nc.vector.tensor_copy(
-                dst[:].rearrange("p (t m b) -> p t m b", t=PACK, b=width),
-                src.rearrange("p (m t b) -> p t m b", t=PACK, b=width),
+                dst[:].rearrange("p (t g i b) -> p g t i b", t=PACK, i=run, b=width),
+                src.rearrange("p (g i t b) -> p g t i b", t=PACK, i=run, b=width),
             )
             return dst
 
-        def project(lst, ww, ws, first_bank, name):
+        spare = tile([P, S], F32, "spare")
+        nc.gpsimd.memset(spare[:], 0.0)
+
+        def window(t, name):
+            if t >= WHOLE:
+                return tile([P, S], F32, name)
+            dst = tile([P, 2 * S], F32, name)
+            nc.scalar.copy(dst[:, S:], spare[:])
+            return dst
+
+        def project(lst, ww, ws, first_bank, name, signs):
+            w_words = deal(ww[:], 2, 8, U8, name + "_ww")
+            scales = keep.tile([P, S], U8, name=name + "_xs", tag=name + "_xs", align_bytes=64)
+            nc.vector.tensor_copy(scales[:], xs[:].indirect(lst[:]))
             words = tile([P, S], U32, name + "_xw")
             nc.vector.tensor_copy(words[:], xw[:].bitcast(U32).indirect(lst[:]))
-            w_words = deal(ww[:], 2, U8, name + "_ww")
-            scales = tile([P, S], U8, name + "_xs")
-            nc.vector.tensor_copy(scales[:], xs[:].indirect(lst[:]))
-            w_scales = deal(ws[:], 1, U8, name + "_ws")
-            rows = []
+            w_scales = deal(ws[:], 1, 16, U8, name + "_ws")
+            rows = [[window(t, "%s%d_%d" % (name, t, k)) for t in range(PACK)] for k in range(len(signs))]
             for t in range(PACK):
                 acc = bank(first_bank + t, [P, S])
                 nc.tensor.matmul_mx(
@@ -117,111 +140,173 @@ def tile_picked_twqpathbdot_none_po_kernel(
                     start=True,
                     stop=True,
                 )
-                row = tile([P, S], F32, "%s%d" % (name, t))
-                nc.scalar.copy(row[:], acc[:])
-                rows.append(row)
+                for row, sign in zip(rows, signs):
+                    nc.scalar.activation(row[t][:, :S], acc[:], COPY, scale=sign)
             return rows
 
-        y = project(l_offs, w1w, w1s, 0, "y")
-        d = project(l_two, w2w, w2s, 4, "d")
+        (y,) = project(l_offs, w1w, w1s, 0, "y", (1.0,))
+        minus_d, d = project(l_two, w2w, w2s, 4, "d", (-1.0, 1.0))
 
         z_words = tile([P, S], U32, "z_words")
         z_scales = tile([P, S], U8, "z_scales")
 
-        def mix(c0, n):
-            ya = tile([P, PACK, n], F32, "ya%d" % c0)
-            yb = tile([P, PACK, n], F32, "yb%d" % c0)
-            sa = tile([P, PACK, n], F32, "sa%d" % c0)
-            sb = tile([P, PACK, n], F32, "sb%d" % c0)
-            top = tile([P, PACK, n], F32, "top%d" % c0)
-            planes = tile([P, PACK, n], BF16, "planes%d" % c0)
-            woven = tile([P, n, PACK], BF16, "woven%d" % c0)
-            for t in range(PACK):
-                nc.vector.tensor_copy(ya[:, t, :], y[t][:].indirect(entries(l1, c0, n)))
-                nc.vector.tensor_copy(yb[:, t, :], y[t][:].indirect(entries(l2, c0, n)))
-            for t in range(PACK + 1):
-                if t < PACK:
-                    nc.vector.tensor_tensor(sa[:, t, :], d[t][:].indirect(entries(l3, c0, n)), ya[:, t, :], ADD)
-                    nc.vector.tensor_tensor(sb[:, t, :], d[t][:].indirect(entries(l4, c0, n)), yb[:, t, :], ADD)
-                if t > 0:
-                    u = t - 1
-                    nc.vector.tensor_tensor(top[:, u, :], sa[:, u, :], sb[:, u, :], MAX)
-                    nc.scalar.activation(planes[:, u, :], top[:, u, :], COPY, scale=gains[:, u : u + 1])
-            nc.scalar.copy(woven[:], planes[:].rearrange("p t j -> p j t"))
-            return woven
+        def turned_sum(dst, parts):
+            for k, part in enumerate(parts):
+                nc.tensor.matmul(dst, part, ident[:], start=k == 0, stop=k == len(parts) - 1, is_transpose=True)
+
+        def fetch(dst, window, lst, c0, n, other=None, op=None):
+            picked = window[:].indirect(entries(lst, c0, n))
+            if other is None:
+                nc.vector.tensor_copy(dst, picked)
+            else:
+                nc.vector.tensor_tensor(dst, picked, other, op)
+
+        woven_z = [tile([P, HALF, PACK], BF16, "woven_z%d" % c0) for c0 in (0, HALF)]
+
+        def held(name, n, tag):
+            if tag is None:
+                return ring.tile([P, n], F32, name=name, tag=name)
+            return keep.tile([P, n], F32, name=name, tag=tag, align_bytes=64)
+
+        def mix(c0, n, tiles, tags, direct=False):
+            blocks = [slice(P * b, P * (b + 1)) for b in range(n // P)]
+            y1, y2, first, minus_second, second_turned, excess = {}, {}, {}, {}, {}, {}
+            for t in tiles:
+                y2[t] = pairs.tile([P, n], F32, name="y2", tag="y2")
+                fetch(y2[t][:], y[t], l2, c0, n)
+            for t in tiles:
+                y1[t] = pairs.tile([P, n], F32, name="y1", tag="y1")
+                fetch(y1[t][:], y[t], l1, c0, n)
+            for t in tiles:
+                minus_second[t] = held("minus_second", n, None)
+                fetch(minus_second[t][:], minus_d[t], l4, c0, n, y2[t][:], SUB)
+            for t in tiles:
+                first[t] = held("first", n, tags.get(("first", t)))
+                fetch(first[t][:], d[t], l3, c0, n, y1[t][:], ADD)
+
+            def weigh(src, t):
+                for c in range(0, n, HALF):
+                    nc.scalar.activation(woven_z[(c0 + c) // HALF][:, :, t], src[:, c : c + HALF], COPY, scale=gains[:, t : t + 1])
+
+            if direct:
+                for t in tiles:
+                    top = held("top", n, tags.get(("top", t)))
+                    nc.vector.scalar_tensor_tensor(top[:], minus_second[t][:], -1.0, first[t][:], MULT, MAX)
+                    weigh(top, t)
+                return
+            for t in tiles:
+                acc = bank(t % 2, [P, n])
+                for blk in blocks:
+                    turned_sum(acc[:, blk], [minus_second[t][:, blk]])
+                second_turned[t] = held("second_turned", n, None)
+                nc.scalar.activation(second_turned[t][:], acc[:], COPY, scale=-1.0)
+            for t in tiles:
+                acc = bank(t % 2, [P, n])
+                for blk in blocks:
+                    turned_sum(acc[:, blk], [minus_second[t][:, blk], first[t][:, blk]])
+                excess[t] = held("excess", n, tags.get(("excess", t)))
+                nc.scalar.activation(excess[t][:], acc[:], RELU)
+                acc = bank(4 + t % 2, [P, n])
+                for blk in blocks:
+                    turned_sum(acc[:, blk], [second_turned[t][:, blk], excess[t][:, blk]])
+                weigh(acc, t)
 
         def quantise(woven, words, scales, c0, n):
             nc.vector.quantize_mx(words[:, c0 : c0 + n].bitcast(FP8X4), scales[:, c0 : c0 + n], woven[:].rearrange("p j t -> p (j t)"))
 
-        woven_z = [mix(*CHUNKS[0])]
-
+        mix(0, S, (0, 1), {})
         dk_scales = tile([P, H], U8, "dk_scales")
         nc.vector.tensor_copy(dk_scales[:], ds[:].indirect(lk[:]))
-        dk_scales_dealt = deal(dk_scales[:], 1, U8, "dk_scales_dealt")
+        dk_scales_dealt = deal(dk_scales[:], 1, 16, U8, "dk_scales_dealt")
         for r in range(4):
             first = 16 * (r // 2) + r % 2
             nc.sync.dma_start(ds_placed[r:P:32, :].bitcast(I32), dk_scales_dealt[first:P:32, :].bitcast(I32))
-        dk_words = tile([P, H], U32, "dk_words")
+
+        mix(0, HALF, (2, 3), {("excess", 2): "top3", ("excess", 3): "top2"})
+        quantise(woven_z[0], z_words, z_scales, 0, HALF)
+        mix(HALF, HALF, (2, 3), {("first", 2): "dk_words", ("top", 2): "top2", ("top", 3): "top3"}, direct=True)
+
+        dk_words = keep.tile([P, H], U32, name="dk_words", tag="dk_words", align_bytes=64)
         nc.vector.tensor_copy(dk_words[:], dw[:].bitcast(U32).indirect(lk[:]))
-        dk = deal(dk_words[:].bitcast(I32), 1, I32, "dk")
+        dk = deal(dk_words[:].bitcast(I32), 1, 4, I32, "dk")
 
         h = [tile([P, S], F32, "h%d" % t) for t in range(PACK)]
-        hs = [tile([P, S], F32, "hs%d" % t) for t in range(PACK)]
+        own = [keep.tile([P, S], F32, name="own", tag="own%d" % t, align_bytes=64) for t in range(PACK)]
 
-        def layer(i):
-            c0, n = CHUNKS[i]
-            quantise(woven_z[i], z_words, z_scales, c0, n)
-            per_bank = 512 // n
-            accs = [bank(2 * i + b, [P, per_bank, n]) for b in range(PACK // per_bank)]
-            for t in range(PACK):
-                nc.tensor.matmul_mx(
-                    accs[t // per_bank][:, t % per_bank, :],
-                    lhsT=dk[:, P * t : P * (t + 1)].bitcast(FP8X4),
-                    lhsT_scale=ds_placed[:, P * t : P * (t + 1)],
-                    rhs=z_words[:, c0 : c0 + n].bitcast(FP8X4),
-                    rhs_scale=z_scales[:, c0 : c0 + n],
-                    start=True,
-                    stop=True,
-                )
-            for t in range(PACK):
-                acc = accs[t // per_bank][:, t % per_bank, :]
-                nc.scalar.activation(hs[t][:, c0 : c0 + n], acc, COPY, scale=0.75 * 0.0625)
-                nc.scalar.activation(h[t][:, c0 : c0 + n], acc, COPY, scale=0.0625)
+        def layer(acc, t, c0, n):
+            nc.tensor.matmul_mx(
+                acc,
+                lhsT=dk[:, P * t : P * (t + 1)].bitcast(FP8X4),
+                lhsT_scale=ds_placed[:, P * t : P * (t + 1)],
+                rhs=z_words[:, c0 : c0 + n].bitcast(FP8X4),
+                rhs_scale=z_scales[:, c0 : c0 + n],
+                start=True,
+                stop=True,
+            )
 
-        for i in range(1, len(CHUNKS)):
-            woven_z.append(mix(*CHUNKS[i]))
-            layer(i - 1)
-        layer(len(CHUNKS) - 1)
+        acc = bank(6, [P, HALF])
+        layer(acc[:], 0, 0, HALF)
+        nc.scalar.activation(h[0][:, :HALF], acc[:], COPY, scale=H_SCALE)
+        quantise(woven_z[1], z_words, z_scales, HALF, HALF)
+        for t in range(PACK):
+            c0 = HALF if t == 0 else 0
+            acc = bank((7 + t) % 8, [P, S - c0])
+            layer(acc[:], t, c0, S - c0)
+            nc.scalar.activation(h[t][:, c0:], acc[:], COPY, scale=H_SCALE)
+            nc.scalar.copy(own[t][:], h[t][:])
 
-        o_words = tile([P, S], U32, "o_words")
         o_scales = tile([P, S], U8, "o_scales")
         out_rows = out_0.rearrange("(p t) j -> p t j", t=PACK)
         out_words = out_1[0].rearrange("p n t -> p (n t)").bitcast(I32)
 
-        def products(c0, n):
-            h6 = tile([P, PACK, n], F32, "h6_%d" % c0)
-            pa = tile([P, PACK, n], F32, "pa%d" % c0)
-            pb = tile([P, PACK, n], F32, "pb%d" % c0)
-            res = tile([P, PACK, n], F32, "res%d" % c0)
-            woven = tile([P, n, PACK], BF16, "owoven%d" % c0)
-            for t in range(PACK):
-                nc.vector.tensor_copy(h6[:, t, :], hs[t][:].indirect(entries(l6, c0, n)))
-                nc.vector.tensor_tensor(pa[:, t, :], h[t][:].indirect(entries(l5, c0, n)), hs[t][:, c0 : c0 + n], MULT)
-            for t in range(PACK):
-                nc.vector.tensor_tensor(pb[:, t, :], h[t][:].indirect(entries(l7, c0, n)), h6[:, t, :], MULT)
-            nc.vector.tensor_tensor(res[:], pa[:], pb[:], ADD)
-            nc.sync.dma_start(out_rows[:, :, c0 : c0 + n], res[:])
-            nc.scalar.copy(woven[:], res[:].rearrange("p t j -> p j t"))
-            return woven
+        blocks = [slice(P * b, P * (b + 1)) for b in range(LAST // P)]
+        res = tile([P, PACK, LAST], F32, "res")
+        woven_o = [keep.tile([P, n, PACK], BF16, name="woven_o", tag="woven_o%d" % c0, align_bytes=64) for c0, n in CHUNKS]
+        for t in range(PACK):
+            h6 = held("h6", LAST, "h6_last" if t == PACK - 1 else None)
+            pa = held("pa", LAST, None)
+            pb = held("pb", LAST, "pa_last" if t == PACK - 2 else None)
+            fetch(h6[:], h[t], l6, 0, LAST)
+            fetch(pa[:], h[t], l5, 0, LAST, own[t][:, :LAST], MULT)
+            fetch(pb[:], h[t], l7, 0, LAST, h6[:], MULT)
+            if t == PACK - 1:
+                nc.vector.tensor_tensor(res[:, t, :], pa[:], pb[:], ADD)
+            else:
+                sums = bank(3 + t % 2, [P, LAST])
+                for blk in blocks:
+                    turned_sum(sums[:, blk], [pa[:, blk], pb[:, blk]])
+                turned = held("turned", LAST, None)
+                nc.scalar.copy(turned[:], sums[:])
+                back = bank(5 + t % 2, [P, LAST])
+                for blk in blocks:
+                    turned_sum(back[:, blk], [turned[:, blk]])
+                nc.scalar.copy(res[:, t, :], back[:])
+            nc.sync.dma_start(out_rows[:, t, :LAST], res[:, t, :])
+        for woven, (c0, n) in zip(woven_o, CHUNKS[:-1]):
+            nc.scalar.copy(woven[:], res[:, :, c0 : c0 + n].rearrange("p t j -> p j t"))
 
-        def hand_on(woven, c0, n):
-            quantise(woven, o_words, o_scales, c0, n)
-            nc.sync.dma_start(out_words[:, c0 : c0 + n], o_words[:, c0 : c0 + n].bitcast(I32))
-
-        woven_o = [products(*CHUNKS[0])]
-        for i in range(1, len(CHUNKS)):
-            woven_o.append(products(*CHUNKS[i]))
-            hand_on(woven_o[i - 1], *CHUNKS[i - 1])
-        hand_on(woven_o[-1], *CHUNKS[-1])
+        o_words = tile([P, S], U32, "o_words")
+        h6_last = keep.tile([P, PACK - 1, P], F32, name="h6_last", tag="h6_last", align_bytes=64)
+        pa = keep.tile([P, PACK, P], F32, name="pa_last", tag="pa_last", align_bytes=64)
+        pb = tile([P, PACK, P], F32, "pb_last")
+        res = tile([P, PACK, P], F32, "res_last")
+        for t in range(PACK):
+            if t == PACK - 1:
+                quantise(woven_o[0], o_words, o_scales, *CHUNKS[0])
+                nc.sync.dma_start(out_words[:, :256], o_words[:, :256].bitcast(I32))
+            h6 = held("h6", P, "woven_o0")[:] if t == PACK - 1 else h6_last[:, t, :]
+            fetch(h6, h[t], l6, LAST, P)
+            fetch(pa[:, t, :], h[t], l5, LAST, P, own[t][:, LAST:], MULT)
+            if t == PACK - 1:
+                nc.vector.tensor_tensor(res[:, :t, :], pa[:, :t, :], pb[:, :t, :], ADD)
+                nc.sync.dma_start(out_rows[:, :t, LAST:], res[:, :t, :])
+            fetch(pb[:, t, :], h[t], l7, LAST, P, h6, MULT)
+        quantise(woven_o[1], o_words, o_scales, *CHUNKS[1])
+        nc.sync.dma_start(out_words[:, 256:LAST], o_words[:, 256:LAST].bitcast(I32))
+        nc.vector.tensor_tensor(res[:, PACK - 1, :], pa[:, PACK - 1, :], pb[:, PACK - 1, :], ADD)
+        nc.sync.dma_start(out_rows[:, PACK - 1, LAST:], res[:, PACK - 1, :])
+        nc.vector.tensor_copy(woven_o[2][:], res[:].rearrange("p t j -> p j t"))
+        quantise(woven_o[2], o_words, o_scales, *CHUNKS[2])
+        nc.sync.dma_start(out_words[:, LAST:], o_words[:, LAST:].bitcast(I32))
         for q in range(4):
             nc.sync.dma_start(out_2[0, 4 * q : 4 * q + 4, :].bitcast(I32), o_scales[32 * q : 32 * q + 4, :].bitcast(I32))

@@ -62,7 +62,7 @@ def tile_picked_twqpathbdot_none_po_kernel(
             return lst[:, c0 // 16 : (c0 + n) // 16]
 
         xs = tile([P, T], U8, "xs")
-        w1s = keep.tile([P, H], U8, name="w1s", tag="d_xs", align_bytes=64)
+        w1s = keep.tile([P, H], U8, name="w1s", tag="d_xw", align_bytes=64)
         w2s = tile([P, H], U8, "w2s")
         ds = tile([P, G], U8, "ds")
         ds_placed = tile([P, H], U8, "ds_placed")
@@ -83,15 +83,15 @@ def tile_picked_twqpathbdot_none_po_kernel(
 
         l_offs = load_list(offs, "l_offs")
         nc.sync.dma_start(w1w[:].bitcast(I32), w1_words[0].bitcast(I32))
-        nc.sync.dma_start(xw[:], x_words[0].rearrange("p n t -> p (n t)").bitcast(I32))
+        nc.sync.dma_start(w2w[:].bitcast(I32), w2_words[0].bitcast(I32))
         l_two = load_list(two, "l_two")
         load_scales(xs, x_scales)
+        nc.sync.dma_start(xw[:], x_words[0].rearrange("p n t -> p (n t)").bitcast(I32))
         load_scales(w1s, w1_scales)
-        nc.sync.dma_start(w2w[:].bitcast(I32), w2_words[0].bitcast(I32))
         load_scales(w2s, w2_scales)
         l2 = load_list(n2, "l2")
-        l4 = load_list(n4, "l4")
         l1 = load_list(n1, "l1")
+        l4 = load_list(n4, "l4")
         l3 = load_list(n3, "l3")
         nc.sync.dma_start(gains[:], gs.rearrange("(p t) o -> p (t o)", t=PACK))
         lk = load_list(k1, "lk")
@@ -123,9 +123,9 @@ def tile_picked_twqpathbdot_none_po_kernel(
 
         def project(lst, ww, ws, first_bank, name, signs):
             w_words = deal(ww[:], 2, 8, U8, name + "_ww")
-            scales = keep.tile([P, S], U8, name=name + "_xs", tag=name + "_xs", align_bytes=64)
+            scales = tile([P, S], U8, name + "_xs")
             nc.vector.tensor_copy(scales[:], xs[:].indirect(lst[:]))
-            words = tile([P, S], U32, name + "_xw")
+            words = keep.tile([P, S], U32, name=name + "_xw", tag=name + "_xw", align_bytes=64)
             nc.vector.tensor_copy(words[:], xw[:].bitcast(U32).indirect(lst[:]))
             w_scales = deal(ws[:], 1, 16, U8, name + "_ws")
             rows = [[window(t, "%s%d_%d" % (name, t, k)) for t in range(PACK)] for k in range(len(signs))]

import math
from contextlib import ExitStack

import concourse.mybir as mybir
from concourse.masks import make_identity

K, T, S, H, G = 512, 1024, 512, 512, 2048
FLOPS = 3 * 2 * K * H * S

F32 = mybir.dt.float32
BF16 = mybir.dt.bfloat16
I32 = mybir.dt.int32
U32 = mybir.dt.uint32
U16 = mybir.dt.uint16
U8 = mybir.dt.uint8
FP8X4 = mybir.dt.float8_e4m3fn_x4
FP4X4 = mybir.dt.float4_e2m1fn_x4
ADD = mybir.AluOpType.add
SUB = mybir.AluOpType.subtract
MAX = mybir.AluOpType.max
MULT = mybir.AluOpType.mult
RELU = mybir.ActivationFunctionType.Relu
COPY = mybir.ActivationFunctionType.Copy

H_SCALE = 0.0625 * math.sqrt(0.75)
P = 128
PACK = 4
CHUNKS = ((0, 256), (256, 128), (384, 128))
LAST = S - P
HALF = S // 2
WHOLE = 2


def tile_picked_twqpathbdot_none_po_kernel(
    tc, x_words, x_scales, w1_words, w1_scales, w2_words, w2_scales, gs, d_words, d_scales,
    offs, two, n1, n2, n3, n4, k1, n5, n6, n7, out_0, out_1, out_2,
):
    nc = tc.nc
    with ExitStack() as ctx:
        lists = ctx.enter_context(tc.tile_pool(name="lists", bufs=1))
        keep = ctx.enter_context(tc.tile_pool(name="keep", bufs=1))
        ring = ctx.enter_context(tc.tile_pool(name="ring", bufs=4))
        pairs = ctx.enter_context(tc.tile_pool(name="pairs", bufs=2))
        psum = ctx.enter_context(tc.psum_pool(name="psum", bufs=1))

        def tile(shape, dtype, name):
            return keep.tile(shape, dtype, name=name, align_bytes=64)

        def bank(b, shape):
            return psum.tile(shape, F32, name="bank%d" % b, tag="bank%d" % b)

        def load_list(src, name):
            dst = lists.tile([P, S // 16], U16, name=name)
            nc.sync.dma_start(dst[:], src)
            return dst

        def load_scales(dst, src):
            for q in range(4):
                nc.sync.dma_start(dst[32 * q : 32 * q + 4, :].bitcast(I32), src[0, 4 * q : 4 * q + 4, :].bitcast(I32))

        def entries(lst, c0, n):
            return lst[:, c0 // 16 : (c0 + n) // 16]

        xs = tile([P, T], U8, "xs")
        w1s = keep.tile([P, H], U8, name="w1s", tag="d_xw", align_bytes=64)
        w2s = tile([P, H], U8, "w2s")
        ds = tile([P, G], U8, "ds")
        ds_placed = tile([P, H], U8, "ds_placed")
        nc.gpsimd.memset(xs[:].bitcast(I32), 0)
        nc.gpsimd.memset(w1s[:].bitcast(I32), 0)
        nc.gpsimd.memset(w2s[:].bitcast(I32), 0)
        nc.gpsimd.memset(ds[:].bitcast(I32), 0)
        nc.gpsimd.memset(ds_placed[:].bitcast(I32), 0)

        ident = tile([P, P], F32, "ident")
        make_identity(nc, ident[:])

        xw = tile([P, T], I32, "xw")
        w1w = tile([P, 2 * H], U8, "w1w")
        w2w = tile([P, 2 * H], U8, "w2w")
        dw = tile([P, G], I32, "dw")
        gains = tile([P, PACK], F32, "gains")

        l_offs = load_list(offs, "l_offs")
        nc.sync.dma_start(w1w[:].bitcast(I32), w1_words[0].bitcast(I32))
        nc.sync.dma_start(w2w[:].bitcast(I32), w2_words[0].bitcast(I32))
        l_two = load_list(two, "l_two")
        load_scales(xs, x_scales)
        nc.sync.dma_start(xw[:], x_words[0].rearrange("p n t -> p (n t)").bitcast(I32))
        load_scales(w1s, w1_scales)
        load_scales(w2s, w2_scales)
        l2 = load_list(n2, "l2")
        l1 = load_list(n1, "l1")
        l4 = load_list(n4, "l4")
        l3 = load_list(n3, "l3")
        nc.sync.dma_start(gains[:], gs.rearrange("(p t) o -> p (t o)", t=PACK))
        lk = load_list(k1, "lk")
        for r in range(4):
            first = 16 * (r // 2) + r % 2
            nc.sync.dma_start(ds[first:P:32, :].bitcast(I32), d_scales[0, r:16:4, :].bitcast(I32))
        nc.sync.dma_start(dw[:], d_words[0].rearrange("p n t -> p (n t)").bitcast(I32))
        l5 = load_list(n5, "l5")
        l6 = load_list(n6, "l6")
        l7 = load_list(n7, "l7")

        def deal(src, width, run, dtype, name):
            dst = keep.tile([P, H * width], dtype, name=name, tag=name, align_bytes=64)
            nc.vector.tensor_copy(
                dst[:].rearrange("p (t g i b) -> p g t i b", t=PACK, i=run, b=width),
                src.rearrange("p (g i t b) -> p g t i b", t=PACK, i=run, b=width),
            )
            return dst

        spare = tile([P, S], F32, "spare")
        nc.gpsimd.memset(spare[:], 0.0)

        def window(t, name):
            if t >= WHOLE:
                return tile([P, S], F32, name)
            dst = tile([P, 2 * S], F32, name)
            nc.scalar.copy(dst[:, S:], spare[:])
            return dst

        def project(lst, ww, ws, first_bank, name, signs):
            w_words = deal(ww[:], 2, 8, U8, name + "_ww")
            scales = tile([P, S], U8, name + "_xs")
            nc.vector.tensor_copy(scales[:], xs[:].indirect(lst[:]))
            words = keep.tile([P, S], U32, name=name + "_xw", tag=name + "_xw", align_bytes=64)
            nc.vector.tensor_copy(words[:], xw[:].bitcast(U32).indirect(lst[:]))
            w_scales = deal(ws[:], 1, 16, U8, name + "_ws")
            rows = [[window(t, "%s%d_%d" % (name, t, k)) for t in range(PACK)] for k in range(len(signs))]
            for t in range(PACK):
                acc = bank(first_bank + t, [P, S])
                nc.tensor.matmul_mx(
                    acc[:],
                    lhsT=w_words[:, 2 * P * t : 2 * P * (t + 1)].bitcast(FP4X4),
                    lhsT_scale=w_scales[:, P * t : P * (t + 1)],
                    rhs=words[:].bitcast(FP8X4),
                    rhs_scale=scales[:],
                    start=True,
                    stop=True,
                )
                for row, sign in zip(rows, signs):
                    nc.scalar.activation(row[t][:, :S], acc[:], COPY, scale=sign)
            return rows

        (y,) = project(l_offs, w1w, w1s, 0, "y", (1.0,))
        minus_d, d = project(l_two, w2w, w2s, 4, "d", (-1.0, 1.0))

        z_words = tile([P, S], U32, "z_words")
        z_scales = tile([P, S], U8, "z_scales")

        def turned_sum(dst, parts):
            for k, part in enumerate(parts):
                nc.tensor.matmul(dst, part, ident[:], start=k == 0, stop=k == len(parts) - 1, is_transpose=True)

        def fetch(dst, window, lst, c0, n, other=None, op=None):
            picked = window[:].indirect(entries(lst, c0, n))
            if other is None:
                nc.vector.tensor_copy(dst, picked)
            else:
                nc.vector.tensor_tensor(dst, picked, other, op)

        woven_z = [tile([P, HALF, PACK], BF16, "woven_z%d" % c0) for c0 in (0, HALF)]

        def held(name, n, tag):
            if tag is None:
                return ring.tile([P, n], F32, name=name, tag=name)
            return keep.tile([P, n], F32, name=name, tag=tag, align_bytes=64)

        def mix(c0, n, tiles, tags, direct=False):
            blocks = [slice(P * b, P * (b + 1)) for b in range(n // P)]
            y1, y2, first, minus_second, second_turned, excess = {}, {}, {}, {}, {}, {}
            for t in tiles:
                y2[t] = pairs.tile([P, n], F32, name="y2", tag="y2")
                fetch(y2[t][:], y[t], l2, c0, n)
            for t in tiles:
                y1[t] = pairs.tile([P, n], F32, name="y1", tag="y1")
                fetch(y1[t][:], y[t], l1, c0, n)
            for t in tiles:
                minus_second[t] = held("minus_second", n, None)
                fetch(minus_second[t][:], minus_d[t], l4, c0, n, y2[t][:], SUB)
            for t in tiles:
                first[t] = held("first", n, tags.get(("first", t)))
                fetch(first[t][:], d[t], l3, c0, n, y1[t][:], ADD)

            def weigh(src, t):
                for c in range(0, n, HALF):
                    nc.scalar.activation(woven_z[(c0 + c) // HALF][:, :, t], src[:, c : c + HALF], COPY, scale=gains[:, t : t + 1])

            if direct:
                for t in tiles:
                    top = held("top", n, tags.get(("top", t)))
                    nc.vector.scalar_tensor_tensor(top[:], minus_second[t][:], -1.0, first[t][:], MULT, MAX)
                    weigh(top, t)
                return
            for t in tiles:
                acc = bank(t % 2, [P, n])
                for blk in blocks:
                    turned_sum(acc[:, blk], [minus_second[t][:, blk]])
                second_turned[t] = held("second_turned", n, None)
                nc.scalar.activation(second_turned[t][:], acc[:], COPY, scale=-1.0)
            for t in tiles:
                acc = bank(t % 2, [P, n])
                for blk in blocks:
                    turned_sum(acc[:, blk], [minus_second[t][:, blk], first[t][:, blk]])
                excess[t] = held("excess", n, tags.get(("excess", t)))
                nc.scalar.activation(excess[t][:], acc[:], RELU)
                acc = bank(4 + t % 2, [P, n])
                for blk in blocks:
                    turned_sum(acc[:, blk], [second_turned[t][:, blk], excess[t][:, blk]])
                weigh(acc, t)

        def quantise(woven, words, scales, c0, n):
            nc.vector.quantize_mx(words[:, c0 : c0 + n].bitcast(FP8X4), scales[:, c0 : c0 + n], woven[:].rearrange("p j t -> p (j t)"))

        mix(0, S, (0, 1), {})
        dk_scales = tile([P, H], U8, "dk_scales")
        nc.vector.tensor_copy(dk_scales[:], ds[:].indirect(lk[:]))
        dk_scales_dealt = deal(dk_scales[:], 1, 16, U8, "dk_scales_dealt")
        for r in range(4):
            first = 16 * (r // 2) + r % 2
            nc.sync.dma_start(ds_placed[r:P:32, :].bitcast(I32), dk_scales_dealt[first:P:32, :].bitcast(I32))

        mix(0, HALF, (2, 3), {("excess", 2): "top3", ("excess", 3): "top2"})
        quantise(woven_z[0], z_words, z_scales, 0, HALF)
        mix(HALF, HALF, (2, 3), {("first", 2): "dk_words", ("top", 2): "top2", ("top", 3): "top3"}, direct=True)

        dk_words = keep.tile([P, H], U32, name="dk_words", tag="dk_words", align_bytes=64)
        nc.vector.tensor_copy(dk_words[:], dw[:].bitcast(U32).indirect(lk[:]))
        dk = deal(dk_words[:].bitcast(I32), 1, 4, I32, "dk")

        h = [tile([P, S], F32, "h%d" % t) for t in range(PACK)]
        own = [keep.tile([P, S], F32, name="own", tag="own%d" % t, align_bytes=64) for t in range(PACK)]

        def layer(acc, t, c0, n):
            nc.tensor.matmul_mx(
                acc,
                lhsT=dk[:, P * t : P * (t + 1)].bitcast(FP8X4),
                lhsT_scale=ds_placed[:, P * t : P * (t + 1)],
                rhs=z_words[:, c0 : c0 + n].bitcast(FP8X4),
                rhs_scale=z_scales[:, c0 : c0 + n],
                start=True,
                stop=True,
            )

        acc = bank(6, [P, HALF])
        layer(acc[:], 0, 0, HALF)
        nc.scalar.activation(h[0][:, :HALF], acc[:], COPY, scale=H_SCALE)
        quantise(woven_z[1], z_words, z_scales, HALF, HALF)
        for t in range(PACK):
            c0 = HALF if t == 0 else 0
            acc = bank((7 + t) % 8, [P, S - c0])
            layer(acc[:], t, c0, S - c0)
            nc.scalar.activation(h[t][:, c0:], acc[:], COPY, scale=H_SCALE)
            nc.scalar.copy(own[t][:], h[t][:])

        o_scales = tile([P, S], U8, "o_scales")
        out_rows = out_0.rearrange("(p t) j -> p t j", t=PACK)
        out_words = out_1[0].rearrange("p n t -> p (n t)").bitcast(I32)

        blocks = [slice(P * b, P * (b + 1)) for b in range(LAST // P)]
        res = tile([P, PACK, LAST], F32, "res")
        woven_o = [keep.tile([P, n, PACK], BF16, name="woven_o", tag="woven_o%d" % c0, align_bytes=64) for c0, n in CHUNKS]
        for t in range(PACK):
            h6 = held("h6", LAST, "h6_last" if t == PACK - 1 else None)
            pa = held("pa", LAST, None)
            pb = held("pb", LAST, "pa_last" if t == PACK - 2 else None)
            fetch(h6[:], h[t], l6, 0, LAST)
            fetch(pa[:], h[t], l5, 0, LAST, own[t][:, :LAST], MULT)
            fetch(pb[:], h[t], l7, 0, LAST, h6[:], MULT)
            if t == PACK - 1:
                nc.vector.tensor_tensor(res[:, t, :], pa[:], pb[:], ADD)
            else:
                sums = bank(3 + t % 2, [P, LAST])
                for blk in blocks:
                    turned_sum(sums[:, blk], [pa[:, blk], pb[:, blk]])
                turned = held("turned", LAST, None)
                nc.scalar.copy(turned[:], sums[:])
                back = bank(5 + t % 2, [P, LAST])
                for blk in blocks:
                    turned_sum(back[:, blk], [turned[:, blk]])
                nc.scalar.copy(res[:, t, :], back[:])
            nc.sync.dma_start(out_rows[:, t, :LAST], res[:, t, :])
        for woven, (c0, n) in zip(woven_o, CHUNKS[:-1]):
            nc.scalar.copy(woven[:], res[:, :, c0 : c0 + n].rearrange("p t j -> p j t"))

        o_words = tile([P, S], U32, "o_words")
        h6_last = keep.tile([P, PACK - 1, P], F32, name="h6_last", tag="h6_last", align_bytes=64)
        pa = keep.tile([P, PACK, P], F32, name="pa_last", tag="pa_last", align_bytes=64)
        pb = tile([P, PACK, P], F32, "pb_last")
        res = tile([P, PACK, P], F32, "res_last")
        for t in range(PACK):
            if t == PACK - 1:
                quantise(woven_o[0], o_words, o_scales, *CHUNKS[0])
                nc.sync.dma_start(out_words[:, :256], o_words[:, :256].bitcast(I32))
            h6 = held("h6", P, "woven_o0")[:] if t == PACK - 1 else h6_last[:, t, :]
            fetch(h6, h[t], l6, LAST, P)
            fetch(pa[:, t, :], h[t], l5, LAST, P, own[t][:, LAST:], MULT)
            if t == PACK - 1:
                nc.vector.tensor_tensor(res[:, :t, :], pa[:, :t, :], pb[:, :t, :], ADD)
                nc.sync.dma_start(out_rows[:, :t, LAST:], res[:, :t, :])
            fetch(pb[:, t, :], h[t], l7, LAST, P, h6, MULT)
        quantise(woven_o[1], o_words, o_scales, *CHUNKS[1])
        nc.sync.dma_start(out_words[:, 256:LAST], o_words[:, 256:LAST].bitcast(I32))
        nc.vector.tensor_tensor(res[:, PACK - 1, :], pa[:, PACK - 1, :], pb[:, PACK - 1, :], ADD)
        nc.sync.dma_start(out_rows[:, PACK - 1, LAST:], res[:, PACK - 1, :])
        nc.vector.tensor_copy(woven_o[2][:], res[:].rearrange("p t j -> p j t"))
        quantise(woven_o[2], o_words, o_scales, *CHUNKS[2])
        nc.sync.dma_start(out_words[:, LAST:], o_words[:, LAST:].bitcast(I32))
        for q in range(4):
            nc.sync.dma_start(out_2[0, 4 * q : 4 * q + 4, :].bitcast(I32), o_scales[32 * q : 32 * q + 4, :].bitcast(I32))
